import numpy as np
import ml_dtypes


def mxq(x, axis, fmt="e4m3"):
    dtype, down = {"e4m3": (ml_dtypes.float8_e4m3fn, 7), "e5m2": (ml_dtypes.float8_e5m2, 14)}[fmt]
    v = np.moveaxis(np.asarray(x, np.float32).astype(ml_dtypes.bfloat16).astype(np.float64), axis, -1)
    blocks = v.reshape(v.shape[:-1] + (-1, 32))
    amax = np.abs(blocks).max(-1, keepdims=True)
    byte = np.maximum(np.where(amax > 0, np.frexp(amax)[1] - 1 + 127, 0) - down, 1)
    scale = np.exp2(byte - 127.0)
    codes = (blocks / scale).astype(np.float32).astype(dtype).astype(np.float64)
    return np.moveaxis((codes * scale).reshape(v.shape), -1, axis)


WIDE = False


def mx_kscale(k):
    if not WIDE:
        return np.ones(k)
    levels = np.array([10, -10, 5, -5, 0])
    if k % 512:
        return np.exp2(np.random.permutation(np.resize(levels, k // 32))).repeat(32)
    a = np.empty((k // 512, 16))
    for p in range(k // 512):
        a[p, :8] = np.random.permutation(np.resize(levels, 8))
        for g in range(8):
            far = levels[np.abs(levels - a[p, g]) >= 10]
            a[p, g + 8] = far[np.random.randint(len(far))]
    return np.exp2(a.ravel()).repeat(32)


def f64(x):
    return np.asarray(x).astype(np.float64)


def striped(idx):
    return np.tile(idx.reshape(-1, 16).T, (8, 1)).astype(np.uint16)


def unstriped(offs):
    return offs[:16].T.reshape(-1).astype(np.int64)


def striped8(idx):
    return np.concatenate([x.reshape(-1, 16).T for x in idx]).astype(np.uint16)


def runs(offs, k):
    lists = np.stack([offs[16 * r : 16 * r + 16].T.reshape(-1) for r in range(8)]).astype(np.int64)
    return lists[np.arange(k) % 512 // 64]


def pack_weight(w):
    k, n = w.shape
    w = f64(np.asarray(w, np.float32).astype(ml_dtypes.bfloat16)).reshape(k // 32, 32, n)
    amax = np.abs(w).max(1)
    byte = np.clip(np.where(amax > 0, np.frexp(amax)[1] - 1 + 127 - 7, 1), 1, 254)
    scaled = (w * np.exp2(127.0 - byte)[:, None, :]).reshape(k, n).astype(np.float32)
    words = np.ascontiguousarray(scaled.reshape(k // 512, 128, 4, n).transpose(0, 1, 3, 2)).astype(ml_dtypes.float8_e4m3fn).view(np.uint8)
    return words, np.ascontiguousarray(byte.astype(np.uint8).reshape(k // 512, 16, n))


def unpack_weight(words, scales):
    g, p, n, _ = words.shape
    vals = np.ascontiguousarray(words).view(ml_dtypes.float8_e4m3fn).astype(np.float64) * np.repeat(np.exp2(scales.astype(np.float64) - 127.0), 8, axis=1)[..., None]
    return vals.transpose(0, 1, 3, 2).reshape(g * 512, n)


K, T, S, G, H, W, C, U = 512, 1024, 512, 2048, 512, 256, 512, 1024


def setup_inputs():
    n = np.random.standard_normal
    s = mx_kscale(K)[:, None]
    packed_xT = pack_weight(n((K, T)) * s)
    packed_dT = pack_weight(n((K, G)) / s)
    perm = np.stack([np.random.permutation(S) for _ in range(8)])
    perm2 = np.random.permutation(U)
    return {
        "x_words": packed_xT[0],
        "x_scales": packed_xT[1],
        "d_words": packed_dT[0],
        "d_scales": packed_dT[1],
        "gs": (np.random.uniform(0.5, 1.5, (K, 1)) / s).astype(np.float32),
        "offs": striped(np.random.permutation(T)[:S]),
        "k1": striped8(np.random.randint(0, G, (8, H))),
        "hz": striped8(np.random.randint(0, T, (8, S))),
        "k2": striped8(np.random.randint(0, G, (8, H))),
        "hy": striped8(np.random.randint(0, T, (8, S))),
        "k3": striped8(np.random.randint(0, G, (8, H))),
        "n1": striped8(perm[:, :W]),
        "n2": striped8(perm[:, W:]),
        "cand": striped(np.random.permutation(T)[:C]),
        "n3": striped(perm2[:S]),
        "n4": striped(perm2[S:]),
        "n5": striped(np.random.permutation(S)),
    }


def reference(x_words, x_scales, d_words, d_scales, gs, offs, k1, hz, k2, hy, k3, n1, n2, cand, n3, n4, n5):
    x_cand = unpack_weight(x_words, x_scales)[:, unstriped(cand)]
    d_k1 = unpack_weight(d_words, d_scales)[np.arange(K)[:, None], runs(k1, K)]
    xq = unpack_weight(x_words, x_scales)[:, unstriped(offs)]
    d_k2 = unpack_weight(d_words, d_scales)[np.arange(K)[:, None], runs(k2, K)]
    x_hz = unpack_weight(x_words, x_scales)[np.arange(K)[:, None], runs(hz, K)]
    d_k3 = unpack_weight(d_words, d_scales)[np.arange(K)[:, None], runs(k3, K)]
    x_hy = unpack_weight(x_words, x_scales)[np.arange(K)[:, None], runs(hy, K)]
    h = 0.0625 * (d_k1.T @ xq + d_k2.T @ x_hz + d_k3.T @ x_hy)
    pa = h[np.arange(H)[:, None], runs(n1, H)]
    pb = h[np.arange(H)[:, None], runs(n2, H)]
    rb = np.maximum(pa, pb)
    ra = pa / (np.abs(pb) + 0.5)
    ua = np.zeros((H, S))
    ua[np.arange(H)[:, None], runs(n1, H)] = ra
    ub = ua.copy()
    ub[np.arange(H)[:, None], runs(n2, H)] = rb
    z = f64(gs) * ub
    s = 0.0625 * ((x_cand.T @ mxq(z, 0, "e4m3")))
    ds = np.zeros((C, S))
    ds[:, unstriped(n5)] = s
    up = np.maximum(s, ds)
    ph = np.zeros((C, U))
    ph[:, unstriped(n3)] = ds
    out = ph.copy()
    out[:, unstriped(n4)] = up
    return out

@@ -1,0 +1,233 @@
+from contextlib import ExitStack
+
+import concourse.mybir as mybir
+
+F32 = mybir.dt.float32
+BF16 = mybir.dt.bfloat16
+U32 = mybir.dt.uint32
+I32 = mybir.dt.int32
+U16 = mybir.dt.uint16
+U8 = mybir.dt.uint8
+FP8X4 = mybir.dt.float8_e4m3fn_x4
+ACT = mybir.ActivationFunctionType
+ALU = mybir.AluOpType
+
+P = 128
+T, G, S, W, U = 1024, 2048, 512, 256, 1024
+FLOPS = 4 * 2 * 512 * 512 * 512
+
+
+def tile_picked_mthhzcratiopagsn_none_p_kernel(tc, x_words, x_scales, d_words, d_scales, gs, offs, k1, hz, k2, hy, k3, n1, n2, cand, n3, n4, n5, out):
+    nc = tc.nc
+    with ExitStack() as ctx:
+        held = ctx.enter_context(tc.tile_pool(name="held", bufs=1))
+        psum = ctx.enter_context(tc.psum_pool(name="psum", bufs=1))
+
+        def load_list(name, src):
+            tile = held.tile(list(src.shape), U16, name=name)
+            nc.sync.dma_start(tile[:], src)
+            return tile
+
+        d_rows = held.tile([P, G], U8, name="d_rows")
+        x_rows = held.tile([P, T], U8, name="x_rows")
+
+        def load_rows(tile, scales):
+            rows = scales[0].bitcast(I32).rearrange("(r e) n -> e r n", e=2)
+            for e in range(2):
+                nc.sync.dma_start(tile[:].bitcast(I32)[e:P:2, :], rows[e].unsqueeze(1).to_broadcast([8, 8, rows.shape[2]]))
+
+        load_rows(d_rows, d_scales)
+        l_k1 = load_list("l_k1", k1)
+        l_k2 = load_list("l_k2", k2)
+        l_k3 = load_list("l_k3", k3)
+        load_rows(x_rows, x_scales)
+        l_offs = load_list("l_offs", offs)
+        l_hz = load_list("l_hz", hz)
+        l_hy = load_list("l_hy", hy)
+        x_tab = held.tile([P, T], U32, name="x_tab")
+        d_tab = held.tile([P, G], U32, name="d_tab")
+        nc.sync.dma_start(x_tab[:].bitcast(I32), x_words[0].rearrange("p n r -> p (n r)").bitcast(I32))
+        nc.sync.dma_start(d_tab[:].bitcast(I32), d_words[0].rearrange("p n r -> p (n r)").bitcast(I32))
+        l_cand = load_list("l_cand", cand)
+        l_n1 = load_list("l_n1", n1)
+        l_n2 = load_list("l_n2", n2)
+        gain = held.tile([P, 4], F32, name="gain")
+        nc.sync.dma_start(gain[:], gs.rearrange("(p t) o -> p (t o)", t=4))
+        l_n5 = load_list("l_n5", n5)
+        l_n3 = load_list("l_n3", n3)
+        l_n4 = load_list("l_n4", n4)
+
+        d_lists = [l_k1, l_k2, l_k3]
+        x_lists = [l_offs, l_hz, l_hy, l_cand]
+
+        d_picked = held.tile([P, 3 * S], U8, name="d_picked", align_bytes=64)
+        d_dealt = held.tile([P, 3 * S], U8, name="d_dealt", align_bytes=64)
+        x_picked = held.tile([P, 3 * S], U8, name="x_picked", align_bytes=64)
+        d_planes = held.tile([P, 3 * S], U8, name="d_planes", align_bytes=64)
+        x_planes = held.tile([P, 3 * S], U8, name="x_planes", align_bytes=64)
+        c_plane = held.tile([P, S], U8, name="c_plane", align_bytes=64)
+        for plane in (d_planes, x_planes, c_plane):
+            nc.gpsimd.memset(plane[:].bitcast(I32)[96:P, :], 0)
+
+        def place_rows(dst, src):
+            nc.sync.dma_start(dst[:].bitcast(I32)[0:112, :], src[:].bitcast(I32)[14:126, :])
+
+        for a in range(3):
+            nc.vector.tensor_copy(d_picked[:, a * S : (a + 1) * S], d_rows[:].indirect(d_lists[a][:]))
+        nc.vector.tensor_copy(x_picked[:, 0:S], x_rows[:].indirect(x_lists[0][:]))
+        nc.vector.tensor_copy(
+            d_dealt[:].rearrange("p (a t m) -> p t a m", a=3, t=4),
+            d_picked[:].rearrange("p (a m t) -> p t a m", a=3, t=4),
+        )
+        place_rows(d_planes, d_dealt)
+        for a in range(1, 3):
+            nc.vector.tensor_copy(x_picked[:, a * S : (a + 1) * S], x_rows[:].indirect(x_lists[a][:]))
+        place_rows(x_planes, x_picked)
+
+        def gather_words(tile, table, offsets):
+            nc.vector.tensor_copy(tile[:], table[:].indirect(offsets[:]))
+
+        def deal(a):
+            nc.vector.tensor_copy(
+                d_codes[a][:].rearrange("p (t c i) -> p c t i", t=4, i=4),
+                raw[a][:].rearrange("p (c i t) -> p c t i", t=4, i=4),
+            )
+
+        d_codes = [held.tile([P, S], U32, name=f"d_codes{a}", align_bytes=64) for a in range(3)]
+        x_codes = [held.tile([P, S], U32, name="x_codes0", align_bytes=64)]
+        gather_words(x_codes[0], x_tab, l_offs)
+        raw = [held.tile([P, S], U32, name=f"d_raw{a}", tag=f"stage{a}", align_bytes=64) for a in range(3)]
+        gather_words(raw[0], d_tab, l_k1)
+        gather_words(raw[1], d_tab, l_k2)
+        deal(0)
+        x_codes.append(held.tile([P, S], U32, name="x_codes1", tag="stage0", align_bytes=64))
+        gather_words(x_codes[1], x_tab, l_hz)
+        deal(1)
+        gather_words(raw[2], d_tab, l_k3)
+        x_codes.append(held.tile([P, S], U32, name="x_codes2", tag="stage1", align_bytes=64))
+        gather_words(x_codes[2], x_tab, l_hy)
+        deal(2)
+        c_picked = held.tile([P, S], U8, name="c_picked", tag="stage2", align_bytes=64)
+        nc.vector.tensor_copy(c_picked[:], x_rows[:].indirect(l_cand[:]))
+        place_rows(c_plane, c_picked)
+
+        h_banks = [psum.tile([P, S], F32, name=f"h_bank{t}") for t in range(4)]
+        for a in range(3):
+            for t in range(4):
+                nc.tensor.matmul_mx(
+                    out=h_banks[t][:],
+                    lhsT=d_codes[a][:, t * P : (t + 1) * P].bitcast(FP8X4),
+                    lhsT_scale=d_planes[:, a * S + t * P : a * S + (t + 1) * P],
+                    rhs=x_codes[a][:].bitcast(FP8X4),
+                    rhs_scale=x_planes[:, a * S : (a + 1) * S],
+                    start=(a == 0),
+                    stop=(a == 2),
+                )
+
+        pa = [held.tile([P, W], F32, name=f"pa{t}") for t in range(4)]
+        pb = [held.tile([P, W], F32, name=f"pb{t}") for t in range(4)]
+        rb = [held.tile([P, W], F32, name=f"rb{t}") for t in range(4)]
+        size = [held.tile([P, W], F32, name=f"size{t}", tag=f"size{t}", align_bytes=64) for t in range(4)]
+        inv = [held.tile([P, W], F32, name=f"inv{t}", tag=f"inv{t}", align_bytes=64) for t in range(4)]
+        ubs = [held.tile([P, S], F32, name=f"ub{t}") for t in range(4)]
+        h, root = {}, {}
+
+        def leave_bank(t):
+            h[t] = held.tile([P, S], F32, name=f"h{t}", tag="h")
+            nc.scalar.activation(h[t][:], h_banks[t][:], ACT.Copy, scale=0.0625)
+
+        def fetch(dst, t, offsets):
+            nc.scalar.activation(dst[t][:], h[t][:].indirect(offsets[:]), ACT.Copy)
+
+        def magnitude(t):
+            nc.scalar.activation(size[t][:], pb[t][:], ACT.Abs)
+
+        def inverse_root(t, tag):
+            root[t] = held.tile([P, W], F32, name=f"root{t}", tag=tag)
+            nc.scalar.activation(root[t][:], size[t][:], ACT.Abs_reciprocal_sqrt, bias=0.5)
+
+        def square(t):
+            nc.scalar.activation(inv[t][:], root[t][:], ACT.Square)
+
+        def larger(t):
+            nc.vector.tensor_tensor(rb[t][:], pa[t][:], pb[t][:], ALU.max)
+
+        def put_rb(t):
+            nc.vector.tensor_copy(ubs[t][:].indirect(l_n2[:]), rb[t][:])
+
+        def put_ra(t):
+            nc.vector.tensor_tensor(ubs[t][:].indirect(l_n1[:]), pa[t][:], inv[t][:], ALU.mult)
+
+        leave_bank(0)
+        fetch(pb, 0, l_n2)
+        nc.vector.tensor_copy(pa[0][:], h[0][:].indirect(l_n1[:]))
+        magnitude(0)
+        larger(0)
+        put_rb(0)
+        leave_bank(1)
+        fetch(pb, 1, l_n2)
+        fetch(pa, 1, l_n1)
+        larger(1)
+        put_rb(1)
+        inverse_root(0, "h")
+        square(0)
+        put_ra(0)
+        for t in range(1, 3):
+            magnitude(t)
+            leave_bank(t + 1)
+            inverse_root(t, f"root{t}")
+            fetch(pb, t + 1, l_n2)
+            fetch(pa, t + 1, l_n1)
+            square(t)
+            larger(t + 1)
+            put_ra(t)
+            put_rb(t + 1)
+        magnitude(3)
+        inverse_root(3, "root3")
+        square(3)
+        put_ra(3)
+        c_codes = held.tile([P, S], U32, name="c_codes", tag="inv3", align_bytes=64)
+        gather_words(c_codes, x_tab, l_cand)
+        pairs = held.tile([P, 2, S, 2], BF16, name="pairs", tag="size2", align_bytes=64)
+        for t in range(4):
+            nc.scalar.activation(pairs[:, t // 2, :, t % 2], ubs[t][:], ACT.Copy, scale=gain[:, t : t + 1])
+        pair_words = pairs[:].rearrange("p u j e -> p (u j e)").bitcast(F32).rearrange("p (u j) -> p j u", u=2)
+        HALF = S // 2
+        z_codes, z_planes, zs = [], [], []
+        for half in range(2):
+            z = held.tile([P, HALF, 2], F32, name=f"z{half}", align_bytes=64)
+            nc.vector.tensor_copy(z[:], pair_words[:, half * HALF : (half + 1) * HALF, :])
+            zs.append(z)
+        for half in range(2):
+            codes = held.tile([P, HALF], U32, name=f"z_codes{half}", align_bytes=64)
+            plane = held.tile([P, HALF], U8, name=f"z_plane{half}", align_bytes=64)
+            nc.vector.quantize_mx(out=codes[:].bitcast(FP8X4), scales=plane[:], in_=zs[half][:].rearrange("p j u -> p (j u)").bitcast(BF16))
+            z_codes.append(codes)
+            z_planes.append(plane)
+
+        for c in range(4):
+            s = held.tile([P, S], F32, name=f"s{c}")
+            for half in range(2):
+                bank = psum.tile([P, HALF], F32, name=f"s_bank{c}_{half}", tag=f"s_bank{(2 * c + half) % 4}")
+                nc.tensor.matmul_mx(
+                    out=bank[:],
+                    lhsT=c_codes[:, c * P : (c + 1) * P].bitcast(FP8X4),
+                    lhsT_scale=c_plane[:, c * P : (c + 1) * P],
+                    rhs=z_codes[half][:].bitcast(FP8X4),
+                    rhs_scale=z_planes[half][:],
+                    start=True,
+                    stop=True,
+                )
+                nc.scalar.activation(s[:, half * HALF : (half + 1) * HALF], bank[:], ACT.Copy, scale=0.0625)
+            ds = held.tile([P, 768], F32, name=f"ds{c}")
+            if c == 0:
+                for half in range(2):
+                    nc.vector.tensor_copy(ds[:].indirect(l_n5[:, half * 16 : (half + 1) * 16]), s[:, half * HALF : (half + 1) * HALF])
+            else:
+                nc.vector.tensor_copy(ds[:].indirect(l_n5[:]), s[:])
+            page = held.tile([P, U], F32, name=f"page{c}")
+            up = held.tile([P, S], F32, name=f"up{c}")
+            nc.vector.tensor_tensor(up[:], s[:], ds[:, 0:S], ALU.max)
+            nc.vector.tensor_copy(page[:].indirect(l_n3[:]), ds[:, 0:S])
+            nc.vector.tensor_copy(page[:].indirect(l_n4[:]), up[:])
+            nc.sync.dma_start(out[c * P : (c + 1) * P, :], page[:])

@@ -1,6 +1,7 @@
 from contextlib import ExitStack
 
 import concourse.mybir as mybir
+from concourse.masks import make_identity
 
 F32 = mybir.dt.float32
 BF16 = mybir.dt.bfloat16
@@ -69,6 +70,9 @@ def tile_picked_mthhzcratiopagsn_none_p_kernel(tc, x_words, x_scales, d_words, d
         for plane in (d_planes, x_planes, c_plane):
             nc.gpsimd.memset(plane[:].bitcast(I32)[96:P, :], 0)
 
+        identity = held.tile([P, P], F32, name="identity")
+        make_identity(nc, identity[:])
+
         def place_rows(dst, src):
             nc.sync.dma_start(dst[:].bitcast(I32)[0:112, :], src[:].bitcast(I32)[14:126, :])
 
@@ -111,7 +115,7 @@ def tile_picked_mthhzcratiopagsn_none_p_kernel(tc, x_words, x_scales, d_words, d
         nc.vector.tensor_copy(c_picked[:], x_rows[:].indirect(l_cand[:]))
         place_rows(c_plane, c_picked)
 
-        h_banks = [psum.tile([P, S], F32, name=f"h_bank{t}") for t in range(4)]
+        h_banks = [psum.tile([P, S], F32, name=f"h_bank{t}", tag=f"h_bank{t}") for t in range(4)]
         for a in range(3):
             for t in range(4):
                 nc.tensor.matmul_mx(
@@ -133,7 +137,7 @@ def tile_picked_mthhzcratiopagsn_none_p_kernel(tc, x_words, x_scales, d_words, d
         h, root = {}, {}
 
         def leave_bank(t):
-            h[t] = held.tile([P, S], F32, name=f"h{t}", tag="h")
+            h[t] = held.tile([P, S], F32, name=f"h{t}", tag="h", align_bytes=64)
             nc.scalar.activation(h[t][:], h_banks[t][:], ACT.Copy, scale=0.0625)
 
         def fetch(dst, t, offsets):
@@ -143,7 +147,7 @@ def tile_picked_mthhzcratiopagsn_none_p_kernel(tc, x_words, x_scales, d_words, d
             nc.scalar.activation(size[t][:], pb[t][:], ACT.Abs)
 
         def inverse_root(t, tag):
-            root[t] = held.tile([P, W], F32, name=f"root{t}", tag=tag)
+            root[t] = held.tile([P, W], F32, name=f"root{t}", tag=tag, align_bytes=64)
             nc.scalar.activation(root[t][:], size[t][:], ACT.Abs_reciprocal_sqrt, bias=0.5)
 
         def square(t):
@@ -173,30 +177,32 @@ def tile_picked_mthhzcratiopagsn_none_p_kernel(tc, x_words, x_scales, d_words, d
         square(0)
         put_ra(0)
         for t in range(1, 3):
-            magnitude(t)
             leave_bank(t + 1)
-            inverse_root(t, f"root{t}")
             fetch(pb, t + 1, l_n2)
             fetch(pa, t + 1, l_n1)
-            square(t)
             larger(t + 1)
-            put_ra(t)
             put_rb(t + 1)
+            magnitude(t)
+            inverse_root(t, f"root{t}")
+            square(t)
+            put_ra(t)
         magnitude(3)
         inverse_root(3, "root3")
         square(3)
         put_ra(3)
-        c_codes = held.tile([P, S], U32, name="c_codes", tag="inv3", align_bytes=64)
-        gather_words(c_codes, x_tab, l_cand)
-        pairs = held.tile([P, 2, S, 2], BF16, name="pairs", tag="size2", align_bytes=64)
-        for t in range(4):
-            nc.scalar.activation(pairs[:, t // 2, :, t % 2], ubs[t][:], ACT.Copy, scale=gain[:, t : t + 1])
-        pair_words = pairs[:].rearrange("p u j e -> p (u j e)").bitcast(F32).rearrange("p (u j) -> p j u", u=2)
+
         HALF = S // 2
+        c_codes = [held.tile([P, HALF], U32, name="c_codes0", tag="inv3", align_bytes=64)]
+        nc.vector.tensor_copy(c_codes[0][:], x_tab[:].indirect(l_cand[:, 0:16]))
+        pairs = [held.tile([P, 2, HALF, 2], BF16, name=f"pairs{half}", tag=("root3", "size3")[half], align_bytes=64) for half in range(2)]
+        for t in range(4):
+            for half in range(2):
+                nc.scalar.activation(pairs[half][:, t // 2, :, t % 2], ubs[t][:, half * HALF : (half + 1) * HALF], ACT.Copy, scale=gain[:, t : t + 1])
         z_codes, z_planes, zs = [], [], []
         for half in range(2):
-            z = held.tile([P, HALF, 2], F32, name=f"z{half}", align_bytes=64)
-            nc.vector.tensor_copy(z[:], pair_words[:, half * HALF : (half + 1) * HALF, :])
+            z = held.tile([P, HALF, 2], F32, name=f"z{half}", tag=f"z{half}", align_bytes=64)
+            pair_words = pairs[half][:].rearrange("p u j e -> p (u j e)").bitcast(F32).rearrange("p (u j) -> p j u", u=2)
+            nc.vector.tensor_copy(z[:], pair_words)
             zs.append(z)
         for half in range(2):
             codes = held.tile([P, HALF], U32, name=f"z_codes{half}", align_bytes=64)
@@ -204,14 +210,17 @@ def tile_picked_mthhzcratiopagsn_none_p_kernel(tc, x_words, x_scales, d_words, d
             nc.vector.quantize_mx(out=codes[:].bitcast(FP8X4), scales=plane[:], in_=zs[half][:].rearrange("p j u -> p (j u)").bitcast(BF16))
             z_codes.append(codes)
             z_planes.append(plane)
+        c_codes.append(held.tile([P, HALF], U32, name="c_codes1", tag="z0", align_bytes=64))
+        nc.vector.tensor_copy(c_codes[1][:], x_tab[:].indirect(l_cand[:, 16:32]))
 
         for c in range(4):
             s = held.tile([P, S], F32, name=f"s{c}")
+            minus_s = held.tile([P, S], F32, name=f"minus_s{c}")
             for half in range(2):
                 bank = psum.tile([P, HALF], F32, name=f"s_bank{c}_{half}", tag=f"s_bank{(2 * c + half) % 4}")
                 nc.tensor.matmul_mx(
                     out=bank[:],
-                    lhsT=c_codes[:, c * P : (c + 1) * P].bitcast(FP8X4),
+                    lhsT=c_codes[c // 2][:, (c % 2) * P : (c % 2 + 1) * P].bitcast(FP8X4),
                     lhsT_scale=c_plane[:, c * P : (c + 1) * P],
                     rhs=z_codes[half][:].bitcast(FP8X4),
                     rhs_scale=z_planes[half][:],
@@ -219,6 +228,7 @@ def tile_picked_mthhzcratiopagsn_none_p_kernel(tc, x_words, x_scales, d_words, d
                     stop=True,
                 )
                 nc.scalar.activation(s[:, half * HALF : (half + 1) * HALF], bank[:], ACT.Copy, scale=0.0625)
+            nc.scalar.activation(minus_s[:], s[:], ACT.Copy, scale=-1.0)
             ds = held.tile([P, 768], F32, name=f"ds{c}")
             if c == 0:
                 for half in range(2):
@@ -226,8 +236,19 @@ def tile_picked_mthhzcratiopagsn_none_p_kernel(tc, x_words, x_scales, d_words, d
             else:
                 nc.vector.tensor_copy(ds[:].indirect(l_n5[:]), s[:])
             page = held.tile([P, U], F32, name=f"page{c}")
-            up = held.tile([P, S], F32, name=f"up{c}")
-            nc.vector.tensor_tensor(up[:], s[:], ds[:, 0:S], ALU.max)
+            turned = psum.tile([P, S], F32, name=f"turned{c}", tag=f"h_bank{2 * (c % 2)}")
+            for b in range(4):
+                cols = slice(b * P, (b + 1) * P)
+                nc.tensor.matmul(turned[:, cols], minus_s[:, cols], identity[:], start=True, stop=False, is_transpose=True)
+                nc.tensor.matmul(turned[:, cols], ds[:, cols], identity[:], start=False, stop=True, is_transpose=True)
+            gain_t = held.tile([P, S], F32, name=f"gain_t{c}")
+            nc.scalar.activation(gain_t[:], turned[:], ACT.Relu)
+            back = psum.tile([P, S], F32, name=f"back{c}", tag=f"h_bank{2 * (c % 2) + 1}")
+            for b in range(4):
+                cols = slice(b * P, (b + 1) * P)
+                nc.tensor.transpose(back[:, cols], gain_t[:, cols], identity[:])
+            excess = held.tile([P, S], F32, name=f"excess{c}")
+            nc.scalar.copy(excess[:], back[:])
             nc.vector.tensor_copy(page[:].indirect(l_n3[:]), ds[:, 0:S])
-            nc.vector.tensor_copy(page[:].indirect(l_n4[:]), up[:])
+            nc.vector.tensor_tensor(page[:].indirect(l_n4[:]), s[:], excess[:], ALU.add)
             nc.sync.dma_start(out[c * P : (c + 1) * P, :], page[:])

@@ -37,14 +37,14 @@ def tile_picked_mthhzcratiopagsn_none_p_kernel(tc, x_words, x_scales, d_words, d
             for e in range(2):
                 nc.sync.dma_start(tile[:].bitcast(I32)[e:P:2, :], rows[e].unsqueeze(1).to_broadcast([8, 8, rows.shape[2]]))
 
-        load_rows(d_rows, d_scales)
-        l_k1 = load_list("l_k1", k1)
-        l_k2 = load_list("l_k2", k2)
-        l_k3 = load_list("l_k3", k3)
         load_rows(x_rows, x_scales)
         l_offs = load_list("l_offs", offs)
+        load_rows(d_rows, d_scales)
+        l_k1 = load_list("l_k1", k1)
         l_hz = load_list("l_hz", hz)
         l_hy = load_list("l_hy", hy)
+        l_k2 = load_list("l_k2", k2)
+        l_k3 = load_list("l_k3", k3)
         x_tab = held.tile([P, T], U32, name="x_tab")
         d_tab = held.tile([P, G], U32, name="d_tab")
         nc.sync.dma_start(x_tab[:].bitcast(I32), x_words[0].rearrange("p n r -> p (n r)").bitcast(I32))
@@ -61,72 +61,74 @@ def tile_picked_mthhzcratiopagsn_none_p_kernel(tc, x_words, x_scales, d_words, d
         d_lists = [l_k1, l_k2, l_k3]
         x_lists = [l_offs, l_hz, l_hy, l_cand]
 
-        d_picked = held.tile([P, 3 * S], U8, name="d_picked", align_bytes=64)
-        d_dealt = held.tile([P, 3 * S], U8, name="d_dealt", align_bytes=64)
-        x_picked = held.tile([P, 3 * S], U8, name="x_picked", align_bytes=64)
-        d_planes = held.tile([P, 3 * S], U8, name="d_planes", align_bytes=64)
-        x_planes = held.tile([P, 3 * S], U8, name="x_planes", align_bytes=64)
+        picked_first = held.tile([P, 2 * S], U8, name="picked_first")
+        picked_rest = held.tile([P, 4 * S], U8, name="picked_rest", tag="picked", align_bytes=64)
+        planes_first = held.tile([P, 2 * S], U8, name="planes_first", align_bytes=64)
+        planes_rest = held.tile([P, 4 * S], U8, name="planes_rest", align_bytes=64)
         c_plane = held.tile([P, S], U8, name="c_plane", align_bytes=64)
-        for plane in (d_planes, x_planes, c_plane):
+        for plane in (planes_first, planes_rest, c_plane):
             nc.gpsimd.memset(plane[:].bitcast(I32)[96:P, :], 0)
-
         identity = held.tile([P, P], F32, name="identity")
         make_identity(nc, identity[:])
 
         def place_rows(dst, src):
             nc.sync.dma_start(dst[:].bitcast(I32)[0:112, :], src[:].bitcast(I32)[14:126, :])
 
+        nc.vector.tensor_copy(picked_first[:, 0:S], x_rows[:].indirect(l_offs[:]))
+        nc.vector.tensor_copy(picked_first[:, S : 2 * S], d_rows[:].indirect(l_k1[:]))
+        place_rows(planes_first, picked_first)
+        for at, (rows, offsets) in enumerate(((x_rows, l_hz), (x_rows, l_hy), (d_rows, l_k2), (d_rows, l_k3))):
+            nc.vector.tensor_copy(picked_rest[:, at * S : (at + 1) * S], rows[:].indirect(offsets[:]))
+        place_rows(planes_rest, picked_rest)
+        x_planes = [planes_first[:, 0:S], planes_rest[:, 0:S], planes_rest[:, S : 2 * S]]
+        d_planes = [planes_first[:, S : 2 * S], planes_rest[:, 2 * S : 3 * S], planes_rest[:, 3 * S : 4 * S]]
+
+        d_codes = [held.tile([P, S], U32, name=f"d_codes{a}", tag=f"d_codes{a}", align_bytes=64) for a in range(3)]
+        token_codes = held.tile([P, S], U32, name="token_codes", align_bytes=64)
+        nc.vector.tensor_copy(token_codes[:], x_tab[:].indirect(l_offs[:]))
         for a in range(3):
-            nc.vector.tensor_copy(d_picked[:, a * S : (a + 1) * S], d_rows[:].indirect(d_lists[a][:]))
-        nc.vector.tensor_copy(x_picked[:, 0:S], x_rows[:].indirect(x_lists[0][:]))
-        nc.vector.tensor_copy(
-            d_dealt[:].rearrange("p (a t m) -> p t a m", a=3, t=4),
-            d_picked[:].rearrange("p (a m t) -> p t a m", a=3, t=4),
-        )
-        place_rows(d_planes, d_dealt)
-        for a in range(1, 3):
-            nc.vector.tensor_copy(x_picked[:, a * S : (a + 1) * S], x_rows[:].indirect(x_lists[a][:]))
-        place_rows(x_planes, x_picked)
-
-        def gather_words(tile, table, offsets):
-            nc.vector.tensor_copy(tile[:], table[:].indirect(offsets[:]))
-
-        def deal(a):
-            nc.vector.tensor_copy(
-                d_codes[a][:].rearrange("p (t c i) -> p c t i", t=4, i=4),
-                raw[a][:].rearrange("p (c i t) -> p c t i", t=4, i=4),
-            )
-
-        d_codes = [held.tile([P, S], U32, name=f"d_codes{a}", align_bytes=64) for a in range(3)]
-        x_codes = [held.tile([P, S], U32, name="x_codes0", align_bytes=64)]
-        gather_words(x_codes[0], x_tab, l_offs)
-        raw = [held.tile([P, S], U32, name=f"d_raw{a}", tag=f"stage{a}", align_bytes=64) for a in range(3)]
-        gather_words(raw[0], d_tab, l_k1)
-        gather_words(raw[1], d_tab, l_k2)
-        deal(0)
-        x_codes.append(held.tile([P, S], U32, name="x_codes1", tag="stage0", align_bytes=64))
-        gather_words(x_codes[1], x_tab, l_hz)
-        deal(1)
-        gather_words(raw[2], d_tab, l_k3)
-        x_codes.append(held.tile([P, S], U32, name="x_codes2", tag="stage1", align_bytes=64))
-        gather_words(x_codes[2], x_tab, l_hy)
-        deal(2)
-        c_picked = held.tile([P, S], U8, name="c_picked", tag="stage2", align_bytes=64)
-        nc.vector.tensor_copy(c_picked[:], x_rows[:].indirect(l_cand[:]))
-        place_rows(c_plane, c_picked)
+            nc.vector.tensor_copy(d_codes[a][:], d_tab[:].indirect(d_lists[a][:]))
+        hashed_codes = held.tile([P, 2 * S], U32, name="hashed_codes", tag="picked", align_bytes=64)
+        x_codes = [token_codes[:], hashed_codes[:, 0:S], hashed_codes[:, S : 2 * S]]
+        for b in range(4):
+            for a in (1, 2):
+                nc.vector.tensor_copy(x_codes[a][:, b * P : (b + 1) * P], x_tab[:].indirect(x_lists[a][:, b * 8 : (b + 1) * 8]))
 
         h_banks = [psum.tile([P, S], F32, name=f"h_bank{t}", tag=f"h_bank{t}") for t in range(4)]
-        for a in range(3):
-            for t in range(4):
-                nc.tensor.matmul_mx(
-                    out=h_banks[t][:],
-                    lhsT=d_codes[a][:, t * P : (t + 1) * P].bitcast(FP8X4),
-                    lhsT_scale=d_planes[:, a * S + t * P : a * S + (t + 1) * P],
-                    rhs=x_codes[a][:].bitcast(FP8X4),
-                    rhs_scale=x_planes[:, a * S : (a + 1) * S],
-                    start=(a == 0),
-                    stop=(a == 2),
-                )
+        h_turned = []
+
+        def turn(t, b):
+            nc.tensor.transpose(h_banks[t][:, b * P : (b + 1) * P], h_turned[b][:, t, :], identity[:])
+
+        sums = [psum.tile([P, S], F32, name=f"sum_bank{b}", tag=f"s_bank{b}") for b in range(4)]
+
+        def product(a, b):
+            nc.tensor.matmul_mx(
+                out=sums[b][:],
+                lhsT=x_codes[a][:, b * P : (b + 1) * P].bitcast(FP8X4),
+                lhsT_scale=x_planes[a][:, b * P : (b + 1) * P],
+                rhs=d_codes[a][:].bitcast(FP8X4),
+                rhs_scale=d_planes[a],
+                start=(a == 0),
+                stop=(a == 2),
+            )
+
+        for b in range(4):
+            product(0, b)
+        for b in range(4):
+            product(1, b)
+            product(2, b)
+            h_turned.append(held.tile([P, 4, P], F32, name=f"h_turned{b}"))
+            dealt = sums[b][:].rearrange("p (m t) -> p t m", t=4)
+            for tiles in (slice(0, 4),) if b < 3 else (slice(0, 1), slice(1, 4)):
+                nc.scalar.activation(h_turned[b][:, tiles, :], dealt[:, tiles, :], ACT.Copy, scale=0.0625)
+        for t in range(4):
+            for b in range(4):
+                turn(t, b)
+
+        c_picked = held.tile([P, S], U8, name="c_picked", tag="d_codes1", align_bytes=64)
+        nc.vector.tensor_copy(c_picked[:], x_rows[:].indirect(l_cand[:]))
+        place_rows(c_plane, c_picked)
 
         pa = [held.tile([P, W], F32, name=f"pa{t}") for t in range(4)]
         pb = [held.tile([P, W], F32, name=f"pb{t}") for t in range(4)]
@@ -138,7 +140,7 @@ def tile_picked_mthhzcratiopagsn_none_p_kernel(tc, x_words, x_scales, d_words, d
 
         def leave_bank(t):
             h[t] = held.tile([P, S], F32, name=f"h{t}", tag="h", align_bytes=64)
-            nc.scalar.activation(h[t][:], h_banks[t][:], ACT.Copy, scale=0.0625)
+            nc.scalar.copy(h[t][:], h_banks[t][:])
 
         def fetch(dst, t, offsets):
             nc.scalar.activation(dst[t][:], h[t][:].indirect(offsets[:]), ACT.Copy)

@@ -14,11 +14,28 @@ ACT = mybir.ActivationFunctionType
 ALU = mybir.AluOpType
 
 P = 128
-T, G, S, W, U = 1024, 2048, 512, 256, 1024
-FLOPS = 4 * 2 * 512 * 512 * 512
+T = 1024
+G = 2048
+S = 512
+W = 256
+U = 1024
+HALF = S // 2
+PACK = 4
+BLOCKS = S // P
+GROUP = 16
+RUNS = P // GROUP
+SHIFT = 14
+MOVED = 112
+LAST_QUADRANT = 96
+DS_COLUMNS = 768
+SIXTEENTH = 0.0625
+
+FLOPS = 4 * 2 * S * S * S
 
 
-def tile_picked_mthhzcratiopagsn_none_p_kernel(tc, x_words, x_scales, d_words, d_scales, gs, offs, k1, hz, k2, hy, k3, n1, n2, cand, n3, n4, n5, out):
+def tile_picked_mthhzcratiopagsn_none_p_kernel(
+    tc, x_words, x_scales, d_words, d_scales, gs, offs, k1, hz, k2, hy, k3, n1, n2, cand, n3, n4, n5, out
+):
     nc = tc.nc
     with ExitStack() as ctx:
         held = ctx.enter_context(tc.tile_pool(name="held", bufs=1))
@@ -29,14 +46,22 @@ def tile_picked_mthhzcratiopagsn_none_p_kernel(tc, x_words, x_scales, d_words, d
             nc.sync.dma_start(tile[:], src)
             return tile
 
-        d_rows = held.tile([P, G], U8, name="d_rows")
-        x_rows = held.tile([P, T], U8, name="x_rows")
+        def entries(offsets, first, count):
+            return offsets[:, first // GROUP : (first + count) // GROUP]
+
+        def gather(dst, window, offsets):
+            nc.vector.tensor_copy(dst, window[:].indirect(offsets))
 
         def load_rows(tile, scales):
             rows = scales[0].bitcast(I32).rearrange("(r e) n -> e r n", e=2)
             for e in range(2):
-                nc.sync.dma_start(tile[:].bitcast(I32)[e:P:2, :], rows[e].unsqueeze(1).to_broadcast([8, 8, rows.shape[2]]))
+                nc.sync.dma_start(tile[:].bitcast(I32)[e:P:2, :], rows[e].unsqueeze(1).to_broadcast([RUNS, GROUP // 2, rows.shape[2]]))
 
+        def load_words(tile, words):
+            nc.sync.dma_start(tile[:].bitcast(I32), words[0].rearrange("p n r -> p (n r)").bitcast(I32))
+
+        d_rows = held.tile([P, G], U8, name="d_rows")
+        x_rows = held.tile([P, T], U8, name="x_rows")
         load_rows(x_rows, x_scales)
         l_offs = load_list("l_offs", offs)
         load_rows(d_rows, d_scales)
@@ -45,97 +70,93 @@ def tile_picked_mthhzcratiopagsn_none_p_kernel(tc, x_words, x_scales, d_words, d
         l_hy = load_list("l_hy", hy)
         l_k2 = load_list("l_k2", k2)
         l_k3 = load_list("l_k3", k3)
-        x_tab = held.tile([P, T], U32, name="x_tab")
-        d_tab = held.tile([P, G], U32, name="d_tab")
-        nc.sync.dma_start(x_tab[:].bitcast(I32), x_words[0].rearrange("p n r -> p (n r)").bitcast(I32))
-        nc.sync.dma_start(d_tab[:].bitcast(I32), d_words[0].rearrange("p n r -> p (n r)").bitcast(I32))
+        x_table = held.tile([P, T], U32, name="x_table")
+        d_table = held.tile([P, G], U32, name="d_table")
+        load_words(x_table, x_words)
+        load_words(d_table, d_words)
         l_cand = load_list("l_cand", cand)
         l_n1 = load_list("l_n1", n1)
         l_n2 = load_list("l_n2", n2)
-        gain = held.tile([P, 4], F32, name="gain")
-        nc.sync.dma_start(gain[:], gs.rearrange("(p t) o -> p (t o)", t=4))
+        gain = held.tile([P, PACK], F32, name="gain")
+        nc.sync.dma_start(gain[:], gs.rearrange("(p t) o -> p (t o)", t=PACK))
         l_n5 = load_list("l_n5", n5)
         l_n3 = load_list("l_n3", n3)
         l_n4 = load_list("l_n4", n4)
 
-        d_lists = [l_k1, l_k2, l_k3]
-        x_lists = [l_offs, l_hz, l_hy, l_cand]
-
-        picked_first = held.tile([P, 2 * S], U8, name="picked_first")
-        picked_rest = held.tile([P, 4 * S], U8, name="picked_rest", tag="picked", align_bytes=64)
-        planes_first = held.tile([P, 2 * S], U8, name="planes_first", align_bytes=64)
-        planes_rest = held.tile([P, 4 * S], U8, name="planes_rest", align_bytes=64)
-        c_plane = held.tile([P, S], U8, name="c_plane", align_bytes=64)
-        for plane in (planes_first, planes_rest, c_plane):
-            nc.gpsimd.memset(plane[:].bitcast(I32)[96:P, :], 0)
+        bytes_first = held.tile([P, 2 * S], U8, name="bytes_first")
+        bytes_rest = held.tile([P, 4 * S], U8, name="bytes_rest", tag="bytes_rest", align_bytes=64)
+        scales_first = held.tile([P, 2 * S], U8, name="scales_first", align_bytes=64)
+        scales_rest = held.tile([P, 4 * S], U8, name="scales_rest", align_bytes=64)
+        cand_scales = held.tile([P, S], U8, name="cand_scales", align_bytes=64)
+        for tile in (scales_first, scales_rest, cand_scales):
+            nc.gpsimd.memset(tile[:].bitcast(I32)[LAST_QUADRANT:P, :], 0)
         identity = held.tile([P, P], F32, name="identity")
         make_identity(nc, identity[:])
 
-        def place_rows(dst, src):
-            nc.sync.dma_start(dst[:].bitcast(I32)[0:112, :], src[:].bitcast(I32)[14:126, :])
+        warm = held.tile([P, 1], F32, name="warm")
+        nc.scalar.activation(warm[:], identity[:, 0:1], ACT.Abs_reciprocal_sqrt, bias=0.5)
 
-        nc.vector.tensor_copy(picked_first[:, 0:S], x_rows[:].indirect(l_offs[:]))
-        nc.vector.tensor_copy(picked_first[:, S : 2 * S], d_rows[:].indirect(l_k1[:]))
-        place_rows(planes_first, picked_first)
+        def place_rows(dst, src):
+            nc.sync.dma_start(dst[:].bitcast(I32)[0:MOVED, :], src[:].bitcast(I32)[SHIFT : SHIFT + MOVED, :])
+
+        gather(bytes_first[:, 0:S], x_rows, l_offs[:])
+        gather(bytes_first[:, S : 2 * S], d_rows, l_k1[:])
+        place_rows(scales_first, bytes_first)
         for at, (rows, offsets) in enumerate(((x_rows, l_hz), (x_rows, l_hy), (d_rows, l_k2), (d_rows, l_k3))):
-            nc.vector.tensor_copy(picked_rest[:, at * S : (at + 1) * S], rows[:].indirect(offsets[:]))
-        place_rows(planes_rest, picked_rest)
-        x_planes = [planes_first[:, 0:S], planes_rest[:, 0:S], planes_rest[:, S : 2 * S]]
-        d_planes = [planes_first[:, S : 2 * S], planes_rest[:, 2 * S : 3 * S], planes_rest[:, 3 * S : 4 * S]]
+            gather(bytes_rest[:, at * S : (at + 1) * S], rows, offsets[:])
+        place_rows(scales_rest, bytes_rest)
+        x_scale = [scales_first[:, 0:S], scales_rest[:, 0:S], scales_rest[:, S : 2 * S]]
+        d_scale = [scales_first[:, S : 2 * S], scales_rest[:, 2 * S : 3 * S], scales_rest[:, 3 * S : 4 * S]]
 
         d_codes = [held.tile([P, S], U32, name=f"d_codes{a}", tag=f"d_codes{a}", align_bytes=64) for a in range(3)]
         token_codes = held.tile([P, S], U32, name="token_codes", align_bytes=64)
-        nc.vector.tensor_copy(token_codes[:], x_tab[:].indirect(l_offs[:]))
-        for a in range(3):
-            nc.vector.tensor_copy(d_codes[a][:], d_tab[:].indirect(d_lists[a][:]))
-        hashed_codes = held.tile([P, 2 * S], U32, name="hashed_codes", tag="picked", align_bytes=64)
+        gather(token_codes[:], x_table, l_offs[:])
+        for codes, offsets in zip(d_codes, (l_k1, l_k2, l_k3)):
+            gather(codes[:], d_table, offsets[:])
+        hashed_codes = held.tile([P, 2 * S], U32, name="hashed_codes", tag="bytes_rest", align_bytes=64)
         x_codes = [token_codes[:], hashed_codes[:, 0:S], hashed_codes[:, S : 2 * S]]
-        for b in range(4):
-            for a in (1, 2):
-                nc.vector.tensor_copy(x_codes[a][:, b * P : (b + 1) * P], x_tab[:].indirect(x_lists[a][:, b * 8 : (b + 1) * 8]))
+        for b in range(BLOCKS):
+            for codes, offsets in zip(x_codes[1:], (l_hz, l_hy)):
+                gather(codes[:, b * P : (b + 1) * P], x_table, entries(offsets, b * P, P))
 
-        h_banks = [psum.tile([P, S], F32, name=f"h_bank{t}", tag=f"h_bank{t}") for t in range(4)]
-        h_turned = []
-
-        def turn(t, b):
-            nc.tensor.transpose(h_banks[t][:, b * P : (b + 1) * P], h_turned[b][:, t, :], identity[:])
-
-        sums = [psum.tile([P, S], F32, name=f"sum_bank{b}", tag=f"s_bank{b}") for b in range(4)]
+        h_banks = [psum.tile([P, S], F32, name=f"h_bank{t}", tag=f"turn_bank{t}") for t in range(PACK)]
+        sums = [psum.tile([P, S], F32, name=f"sum_bank{b}", tag=f"product_bank{b}") for b in range(BLOCKS)]
 
         def product(a, b):
             nc.tensor.matmul_mx(
                 out=sums[b][:],
                 lhsT=x_codes[a][:, b * P : (b + 1) * P].bitcast(FP8X4),
-                lhsT_scale=x_planes[a][:, b * P : (b + 1) * P],
+                lhsT_scale=x_scale[a][:, b * P : (b + 1) * P],
                 rhs=d_codes[a][:].bitcast(FP8X4),
-                rhs_scale=d_planes[a],
+                rhs_scale=d_scale[a],
                 start=(a == 0),
                 stop=(a == 2),
             )
 
-        for b in range(4):
+        h_turned = []
+        for b in range(BLOCKS):
             product(0, b)
-        for b in range(4):
+        for b in range(BLOCKS):
             product(1, b)
             product(2, b)
-            h_turned.append(held.tile([P, 4, P], F32, name=f"h_turned{b}"))
-            dealt = sums[b][:].rearrange("p (m t) -> p t m", t=4)
-            for tiles in (slice(0, 4),) if b < 3 else (slice(0, 1), slice(1, 4)):
-                nc.scalar.activation(h_turned[b][:, tiles, :], dealt[:, tiles, :], ACT.Copy, scale=0.0625)
-        for t in range(4):
-            for b in range(4):
-                turn(t, b)
+            h_turned.append(held.tile([P, PACK, P], F32, name=f"h_turned{b}"))
+            by_tile = sums[b][:].rearrange("p (m t) -> p t m", t=PACK)
+            for tiles in (slice(0, PACK),) if b < BLOCKS - 1 else (slice(0, 1), slice(1, PACK)):
+                nc.scalar.activation(h_turned[b][:, tiles, :], by_tile[:, tiles, :], ACT.Copy, scale=SIXTEENTH)
+        for t in range(PACK):
+            for b in range(BLOCKS):
+                nc.tensor.transpose(h_banks[t][:, b * P : (b + 1) * P], h_turned[b][:, t, :], identity[:])
 
-        c_picked = held.tile([P, S], U8, name="c_picked", tag="d_codes1", align_bytes=64)
-        nc.vector.tensor_copy(c_picked[:], x_rows[:].indirect(l_cand[:]))
-        place_rows(c_plane, c_picked)
+        cand_bytes = held.tile([P, S], U8, name="cand_bytes", tag="d_codes1", align_bytes=64)
+        gather(cand_bytes[:], x_rows, l_cand[:])
+        place_rows(cand_scales, cand_bytes)
 
-        pa = [held.tile([P, W], F32, name=f"pa{t}") for t in range(4)]
-        pb = [held.tile([P, W], F32, name=f"pb{t}") for t in range(4)]
-        rb = [held.tile([P, W], F32, name=f"rb{t}") for t in range(4)]
-        size = [held.tile([P, W], F32, name=f"size{t}", tag=f"size{t}", align_bytes=64) for t in range(4)]
-        inv = [held.tile([P, W], F32, name=f"inv{t}", tag=f"inv{t}", align_bytes=64) for t in range(4)]
-        ubs = [held.tile([P, S], F32, name=f"ub{t}") for t in range(4)]
+        pa = [held.tile([P, W], F32, name=f"pa{t}") for t in range(PACK)]
+        pb = [held.tile([P, W], F32, name=f"pb{t}") for t in range(PACK)]
+        rb = [held.tile([P, W], F32, name=f"rb{t}") for t in range(PACK)]
+        size = [held.tile([P, W], F32, name=f"size{t}", tag=f"size{t}", align_bytes=64) for t in range(PACK)]
+        inverse = [held.tile([P, W], F32, name=f"inverse{t}", tag=f"inverse{t}", align_bytes=64) for t in range(PACK)]
+        ub = [held.tile([P, S], F32, name=f"ub{t}") for t in range(PACK)]
         h, root = {}, {}
 
         def leave_bank(t):
@@ -148,107 +169,109 @@ def tile_picked_mthhzcratiopagsn_none_p_kernel(tc, x_words, x_scales, d_words, d
         def magnitude(t):
             nc.scalar.activation(size[t][:], pb[t][:], ACT.Abs)
 
-        def inverse_root(t, tag):
-            root[t] = held.tile([P, W], F32, name=f"root{t}", tag=tag, align_bytes=64)
+        def inverse_root(t):
+            root[t] = held.tile([P, W], F32, name=f"root{t}", tag=f"root{t}", align_bytes=64)
             nc.scalar.activation(root[t][:], size[t][:], ACT.Abs_reciprocal_sqrt, bias=0.5)
 
         def square(t):
-            nc.scalar.activation(inv[t][:], root[t][:], ACT.Square)
+            nc.scalar.activation(inverse[t][:], root[t][:], ACT.Square)
 
         def larger(t):
             nc.vector.tensor_tensor(rb[t][:], pa[t][:], pb[t][:], ALU.max)
 
         def put_rb(t):
-            nc.vector.tensor_copy(ubs[t][:].indirect(l_n2[:]), rb[t][:])
+            nc.vector.tensor_copy(ub[t][:].indirect(l_n2[:]), rb[t][:])
 
         def put_ra(t):
-            nc.vector.tensor_tensor(ubs[t][:].indirect(l_n1[:]), pa[t][:], inv[t][:], ALU.mult)
+            nc.vector.tensor_tensor(ub[t][:].indirect(l_n1[:]), pa[t][:], inverse[t][:], ALU.mult)
 
+        last = PACK - 1
         leave_bank(0)
         fetch(pb, 0, l_n2)
-        nc.vector.tensor_copy(pa[0][:], h[0][:].indirect(l_n1[:]))
-        magnitude(0)
+        gather(pa[0][:], h[0], l_n1[:])
         larger(0)
         put_rb(0)
-        leave_bank(1)
-        fetch(pb, 1, l_n2)
-        fetch(pa, 1, l_n1)
-        larger(1)
-        put_rb(1)
-        inverse_root(0, "h")
-        square(0)
-        put_ra(0)
-        for t in range(1, 3):
+        for t in range(last):
+            magnitude(t)
             leave_bank(t + 1)
+            inverse_root(t)
             fetch(pb, t + 1, l_n2)
             fetch(pa, t + 1, l_n1)
-            larger(t + 1)
-            put_rb(t + 1)
-            magnitude(t)
-            inverse_root(t, f"root{t}")
             square(t)
+            larger(t + 1)
             put_ra(t)
-        magnitude(3)
-        inverse_root(3, "root3")
-        square(3)
-        put_ra(3)
+            put_rb(t + 1)
+        magnitude(last)
+        inverse_root(last)
+        square(last)
+        put_ra(last)
 
-        HALF = S // 2
-        c_codes = [held.tile([P, HALF], U32, name="c_codes0", tag="inv3", align_bytes=64)]
-        nc.vector.tensor_copy(c_codes[0][:], x_tab[:].indirect(l_cand[:, 0:16]))
-        pairs = [held.tile([P, 2, HALF, 2], BF16, name=f"pairs{half}", tag=("root3", "size3")[half], align_bytes=64) for half in range(2)]
-        for t in range(4):
+        cand_codes = [held.tile([P, HALF], U32, name="cand_codes0", tag=f"inverse{last}", align_bytes=64)]
+        gather(cand_codes[0][:], x_table, entries(l_cand, 0, HALF))
+        pairs = [
+            held.tile([P, 2, HALF, 2], BF16, name=f"pairs{half}", tag=tag, align_bytes=64)
+            for half, tag in enumerate((f"root{last}", f"size{last}"))
+        ]
+        for t in range(PACK):
             for half in range(2):
-                nc.scalar.activation(pairs[half][:, t // 2, :, t % 2], ubs[t][:, half * HALF : (half + 1) * HALF], ACT.Copy, scale=gain[:, t : t + 1])
-        z_codes, z_planes, zs = [], [], []
+                nc.scalar.activation(
+                    pairs[half][:, t // 2, :, t % 2], ub[t][:, half * HALF : (half + 1) * HALF], ACT.Copy, scale=gain[:, t : t + 1]
+                )
+        z, z_codes, z_scales = [], [], []
         for half in range(2):
-            z = held.tile([P, HALF, 2], F32, name=f"z{half}", tag=f"z{half}", align_bytes=64)
-            pair_words = pairs[half][:].rearrange("p u j e -> p (u j e)").bitcast(F32).rearrange("p (u j) -> p j u", u=2)
-            nc.vector.tensor_copy(z[:], pair_words)
-            zs.append(z)
+            z.append(held.tile([P, HALF, 2], F32, name=f"z{half}", tag=f"z{half}", align_bytes=64))
+            words = pairs[half][:].rearrange("p u j e -> p (u j e)").bitcast(F32).rearrange("p (u j) -> p j u", u=2)
+            nc.vector.tensor_copy(z[half][:], words)
         for half in range(2):
-            codes = held.tile([P, HALF], U32, name=f"z_codes{half}", align_bytes=64)
-            plane = held.tile([P, HALF], U8, name=f"z_plane{half}", align_bytes=64)
-            nc.vector.quantize_mx(out=codes[:].bitcast(FP8X4), scales=plane[:], in_=zs[half][:].rearrange("p j u -> p (j u)").bitcast(BF16))
-            z_codes.append(codes)
-            z_planes.append(plane)
-        c_codes.append(held.tile([P, HALF], U32, name="c_codes1", tag="z0", align_bytes=64))
-        nc.vector.tensor_copy(c_codes[1][:], x_tab[:].indirect(l_cand[:, 16:32]))
+            z_codes.append(held.tile([P, HALF], U32, name=f"z_codes{half}", tag=f"z_codes{half}", align_bytes=64))
+            z_scales.append(held.tile([P, HALF], U8, name=f"z_scales{half}", tag=f"z_scales{half}", align_bytes=64))
+            nc.vector.quantize_mx(
+                out=z_codes[half][:].bitcast(FP8X4),
+                scales=z_scales[half][:],
+                in_=z[half][:].rearrange("p j u -> p (j u)").bitcast(BF16),
+            )
+        cand_codes.append(held.tile([P, HALF], U32, name="cand_codes1", tag="z0", align_bytes=64))
+        gather(cand_codes[1][:], x_table, entries(l_cand, HALF, HALF))
 
-        for c in range(4):
+        scores, sent = [], []
+        for c in range(BLOCKS):
             s = held.tile([P, S], F32, name=f"s{c}")
-            minus_s = held.tile([P, S], F32, name=f"minus_s{c}")
             for half in range(2):
-                bank = psum.tile([P, HALF], F32, name=f"s_bank{c}_{half}", tag=f"s_bank{(2 * c + half) % 4}")
+                bank = psum.tile([P, HALF], F32, name=f"s_bank{c}_{half}", tag=f"product_bank{(2 * c + half) % BLOCKS}")
                 nc.tensor.matmul_mx(
                     out=bank[:],
-                    lhsT=c_codes[c // 2][:, (c % 2) * P : (c % 2 + 1) * P].bitcast(FP8X4),
-                    lhsT_scale=c_plane[:, c * P : (c + 1) * P],
+                    lhsT=cand_codes[c // 2][:, (c % 2) * P : (c % 2 + 1) * P].bitcast(FP8X4),
+                    lhsT_scale=cand_scales[:, c * P : (c + 1) * P],
                     rhs=z_codes[half][:].bitcast(FP8X4),
-                    rhs_scale=z_planes[half][:],
+                    rhs_scale=z_scales[half][:],
                     start=True,
                     stop=True,
                 )
-                nc.scalar.activation(s[:, half * HALF : (half + 1) * HALF], bank[:], ACT.Copy, scale=0.0625)
+                nc.scalar.activation(s[:, half * HALF : (half + 1) * HALF], bank[:], ACT.Copy, scale=SIXTEENTH)
+            ds = held.tile([P, DS_COLUMNS], F32, name=f"ds{c}")
+            width = HALF if c == 0 else S
+            for first in range(0, S, width):
+                nc.vector.tensor_copy(ds[:].indirect(entries(l_n5, first, width)), s[:, first : first + width])
+            scores.append(s)
+            sent.append(ds)
+
+        page_tags = ("z_codes1", "z_scales1", "z0", "last_page")
+        for c in range(BLOCKS):
+            s, ds = scores[c], sent[c]
+            minus_s = held.tile([P, S], F32, name=f"minus_s{c}")
             nc.scalar.activation(minus_s[:], s[:], ACT.Copy, scale=-1.0)
-            ds = held.tile([P, 768], F32, name=f"ds{c}")
-            if c == 0:
-                for half in range(2):
-                    nc.vector.tensor_copy(ds[:].indirect(l_n5[:, half * 16 : (half + 1) * 16]), s[:, half * HALF : (half + 1) * HALF])
-            else:
-                nc.vector.tensor_copy(ds[:].indirect(l_n5[:]), s[:])
-            page = held.tile([P, U], F32, name=f"page{c}")
-            turned = psum.tile([P, S], F32, name=f"turned{c}", tag=f"h_bank{2 * (c % 2)}")
-            for b in range(4):
+            page = held.tile([P, U], F32, name=f"page{c}", tag=page_tags[c], align_bytes=64)
+            difference = psum.tile([P, S], F32, name=f"difference{c}", tag=f"turn_bank{2 * (c % 2)}")
+            for b in range(BLOCKS):
                 cols = slice(b * P, (b + 1) * P)
-                nc.tensor.matmul(turned[:, cols], minus_s[:, cols], identity[:], start=True, stop=False, is_transpose=True)
-                nc.tensor.matmul(turned[:, cols], ds[:, cols], identity[:], start=False, stop=True, is_transpose=True)
-            gain_t = held.tile([P, S], F32, name=f"gain_t{c}")
-            nc.scalar.activation(gain_t[:], turned[:], ACT.Relu)
-            back = psum.tile([P, S], F32, name=f"back{c}", tag=f"h_bank{2 * (c % 2) + 1}")
-            for b in range(4):
+                nc.tensor.matmul(difference[:, cols], minus_s[:, cols], identity[:], start=True, stop=False, is_transpose=True)
+                nc.tensor.matmul(difference[:, cols], ds[:, cols], identity[:], start=False, stop=True, is_transpose=True)
+            excess_turned = held.tile([P, S], F32, name=f"excess_turned{c}")
+            nc.scalar.activation(excess_turned[:], difference[:], ACT.Relu)
+            back = psum.tile([P, S], F32, name=f"back{c}", tag=f"turn_bank{2 * (c % 2) + 1}")
+            for b in range(BLOCKS):
                 cols = slice(b * P, (b + 1) * P)
-                nc.tensor.transpose(back[:, cols], gain_t[:, cols], identity[:])
+                nc.tensor.transpose(back[:, cols], excess_turned[:, cols], identity[:])
             excess = held.tile([P, S], F32, name=f"excess{c}")
             nc.scalar.copy(excess[:], back[:])
             nc.vector.tensor_copy(page[:].indirect(l_n3[:]), ds[:, 0:S])

from contextlib import ExitStack

import concourse.mybir as mybir
from concourse.masks import make_identity

F32 = mybir.dt.float32
BF16 = mybir.dt.bfloat16
U32 = mybir.dt.uint32
I32 = mybir.dt.int32
U16 = mybir.dt.uint16
U8 = mybir.dt.uint8
FP8X4 = mybir.dt.float8_e4m3fn_x4
ACT = mybir.ActivationFunctionType
ALU = mybir.AluOpType

P = 128
T = 1024
G = 2048
S = 512
W = 256
U = 1024
HALF = S // 2
PACK = 4
BLOCKS = S // P
GROUP = 16
RUNS = P // GROUP
SHIFT = 14
MOVED = 112
LAST_QUADRANT = 96
DS_COLUMNS = 768
SIXTEENTH = 0.0625

FLOPS = 4 * 2 * S * S * S


def tile_picked_mthhzcratiopagsn_none_p_kernel(
    tc, x_words, x_scales, d_words, d_scales, gs, offs, k1, hz, k2, hy, k3, n1, n2, cand, n3, n4, n5, out
):
    nc = tc.nc
    with ExitStack() as ctx:
        held = ctx.enter_context(tc.tile_pool(name="held", bufs=1))
        psum = ctx.enter_context(tc.psum_pool(name="psum", bufs=1))

        def load_list(name, src):
            tile = held.tile(list(src.shape), U16, name=name)
            nc.sync.dma_start(tile[:], src)
            return tile

        def entries(offsets, first, count):
            return offsets[:, first // GROUP : (first + count) // GROUP]

        def gather(dst, window, offsets):
            nc.vector.tensor_copy(dst, window[:].indirect(offsets))

        def load_rows(tile, scales):
            rows = scales[0].bitcast(I32).rearrange("(r e) n -> e r n", e=2)
            for e in range(2):
                nc.sync.dma_start(tile[:].bitcast(I32)[e:P:2, :], rows[e].unsqueeze(1).to_broadcast([RUNS, GROUP // 2, rows.shape[2]]))

        def load_words(tile, words):
            nc.sync.dma_start(tile[:].bitcast(I32), words[0].rearrange("p n r -> p (n r)").bitcast(I32))

        d_rows = held.tile([P, G], U8, name="d_rows")
        x_rows = held.tile([P, T], U8, name="x_rows")
        load_rows(x_rows, x_scales)
        l_offs = load_list("l_offs", offs)
        load_rows(d_rows, d_scales)
        l_k1 = load_list("l_k1", k1)
        l_hz = load_list("l_hz", hz)
        l_hy = load_list("l_hy", hy)
        l_k2 = load_list("l_k2", k2)
        l_k3 = load_list("l_k3", k3)
        x_table = held.tile([P, T], U32, name="x_table")
        d_table = held.tile([P, G], U32, name="d_table")
        load_words(x_table, x_words)
        load_words(d_table, d_words)
        l_cand = load_list("l_cand", cand)
        l_n1 = load_list("l_n1", n1)
        l_n2 = load_list("l_n2", n2)
        gain = held.tile([P, PACK], F32, name="gain")
        nc.sync.dma_start(gain[:], gs.rearrange("(p t) o -> p (t o)", t=PACK))
        l_n5 = load_list("l_n5", n5)
        l_n3 = load_list("l_n3", n3)
        l_n4 = load_list("l_n4", n4)

        bytes_first = held.tile([P, 2 * S], U8, name="bytes_first")
        bytes_rest = held.tile([P, 4 * S], U8, name="bytes_rest", tag="bytes_rest", align_bytes=64)
        scales_first = held.tile([P, 2 * S], U8, name="scales_first", align_bytes=64)
        scales_rest = held.tile([P, 4 * S], U8, name="scales_rest", align_bytes=64)
        cand_scales = held.tile([P, S], U8, name="cand_scales", align_bytes=64)
        for tile in (scales_first, scales_rest, cand_scales):
            nc.gpsimd.memset(tile[:].bitcast(I32)[LAST_QUADRANT:P, :], 0)
        identity = held.tile([P, P], F32, name="identity")
        make_identity(nc, identity[:])

        warm = held.tile([P, 1], F32, name="warm")
        nc.scalar.activation(warm[:], identity[:, 0:1], ACT.Abs_reciprocal_sqrt, bias=0.5)

        def place_rows(dst, src):
            nc.sync.dma_start(dst[:].bitcast(I32)[0:MOVED, :], src[:].bitcast(I32)[SHIFT : SHIFT + MOVED, :])

        gather(bytes_first[:, 0:S], x_rows, l_offs[:])
        gather(bytes_first[:, S : 2 * S], d_rows, l_k1[:])
        place_rows(scales_first, bytes_first)
        for at, (rows, offsets) in enumerate(((x_rows, l_hz), (x_rows, l_hy), (d_rows, l_k2), (d_rows, l_k3))):
            gather(bytes_rest[:, at * S : (at + 1) * S], rows, offsets[:])
        place_rows(scales_rest, bytes_rest)
        x_scale = [scales_first[:, 0:S], scales_rest[:, 0:S], scales_rest[:, S : 2 * S]]
        d_scale = [scales_first[:, S : 2 * S], scales_rest[:, 2 * S : 3 * S], scales_rest[:, 3 * S : 4 * S]]

        d_codes = [held.tile([P, S], U32, name=f"d_codes{a}", tag=f"d_codes{a}", align_bytes=64) for a in range(3)]
        token_codes = held.tile([P, S], U32, name="token_codes", align_bytes=64)
        gather(token_codes[:], x_table, l_offs[:])
        for codes, offsets in zip(d_codes, (l_k1, l_k2, l_k3)):
            gather(codes[:], d_table, offsets[:])
        hashed_codes = held.tile([P, 2 * S], U32, name="hashed_codes", tag="bytes_rest", align_bytes=64)
        x_codes = [token_codes[:], hashed_codes[:, 0:S], hashed_codes[:, S : 2 * S]]
        for b in range(BLOCKS):
            for codes, offsets in zip(x_codes[1:], (l_hz, l_hy)):
                gather(codes[:, b * P : (b + 1) * P], x_table, entries(offsets, b * P, P))

        h_banks = [psum.tile([P, S], F32, name=f"h_bank{t}", tag=f"turn_bank{t}") for t in range(PACK)]
        sums = [psum.tile([P, S], F32, name=f"sum_bank{b}", tag=f"product_bank{b}") for b in range(BLOCKS)]

        def product(a, b):
            nc.tensor.matmul_mx(
                out=sums[b][:],
                lhsT=x_codes[a][:, b * P : (b + 1) * P].bitcast(FP8X4),
                lhsT_scale=x_scale[a][:, b * P : (b + 1) * P],
                rhs=d_codes[a][:].bitcast(FP8X4),
                rhs_scale=d_scale[a],
                start=(a == 0),
                stop=(a == 2),
            )

        h_turned = []
        for b in range(BLOCKS):
            product(0, b)
        for b in range(BLOCKS):
            product(1, b)
            product(2, b)
            h_turned.append(held.tile([P, PACK, P], F32, name=f"h_turned{b}"))
            by_tile = sums[b][:].rearrange("p (m t) -> p t m", t=PACK)
            for tiles in (slice(0, PACK),) if b < BLOCKS - 1 else (slice(0, 1), slice(1, PACK)):
                nc.scalar.activation(h_turned[b][:, tiles, :], by_tile[:, tiles, :], ACT.Copy, scale=SIXTEENTH)
        for t in range(PACK):
            for b in range(BLOCKS):
                nc.tensor.transpose(h_banks[t][:, b * P : (b + 1) * P], h_turned[b][:, t, :], identity[:])

        cand_bytes = held.tile([P, S], U8, name="cand_bytes", tag="d_codes1", align_bytes=64)
        gather(cand_bytes[:], x_rows, l_cand[:])
        place_rows(cand_scales, cand_bytes)

        pa = [held.tile([P, W], F32, name=f"pa{t}") for t in range(PACK)]
        pb = [held.tile([P, W], F32, name=f"pb{t}") for t in range(PACK)]
        rb = [held.tile([P, W], F32, name=f"rb{t}") for t in range(PACK)]
        size = [held.tile([P, W], F32, name=f"size{t}", tag=f"size{t}", align_bytes=64) for t in range(PACK)]
        inverse = [held.tile([P, W], F32, name=f"inverse{t}", tag=f"inverse{t}", align_bytes=64) for t in range(PACK)]
        ub = [held.tile([P, S], F32, name=f"ub{t}") for t in range(PACK)]
        h, root = {}, {}

        def leave_bank(t):
            h[t] = held.tile([P, S], F32, name=f"h{t}", tag="h", align_bytes=64)
            nc.scalar.copy(h[t][:], h_banks[t][:])

        def fetch(dst, t, offsets):
            nc.scalar.activation(dst[t][:], h[t][:].indirect(offsets[:]), ACT.Copy)

        def magnitude(t):
            nc.scalar.activation(size[t][:], pb[t][:], ACT.Abs)

        def inverse_root(t):
            root[t] = held.tile([P, W], F32, name=f"root{t}", tag=f"root{t}", align_bytes=64)
            nc.scalar.activation(root[t][:], size[t][:], ACT.Abs_reciprocal_sqrt, bias=0.5)

        def square(t):
            nc.scalar.activation(inverse[t][:], root[t][:], ACT.Square)

        def larger(t):
            nc.vector.tensor_tensor(rb[t][:], pa[t][:], pb[t][:], ALU.max)

        def put_rb(t):
            nc.vector.tensor_copy(ub[t][:].indirect(l_n2[:]), rb[t][:])

        def put_ra(t):
            nc.vector.tensor_tensor(ub[t][:].indirect(l_n1[:]), pa[t][:], inverse[t][:], ALU.mult)

        last = PACK - 1
        leave_bank(0)
        fetch(pb, 0, l_n2)
        gather(pa[0][:], h[0], l_n1[:])
        larger(0)
        put_rb(0)
        for t in range(last):
            magnitude(t)
            leave_bank(t + 1)
            inverse_root(t)
            fetch(pb, t + 1, l_n2)
            fetch(pa, t + 1, l_n1)
            square(t)
            larger(t + 1)
            put_ra(t)
            put_rb(t + 1)
        magnitude(last)
        inverse_root(last)
        square(last)
        put_ra(last)

        cand_codes = [held.tile([P, HALF], U32, name="cand_codes0", tag=f"inverse{last}", align_bytes=64)]
        gather(cand_codes[0][:], x_table, entries(l_cand, 0, HALF))
        pairs = [
            held.tile([P, 2, HALF, 2], BF16, name=f"pairs{half}", tag=tag, align_bytes=64)
            for half, tag in enumerate((f"root{last}", f"size{last}"))
        ]
        for t in range(PACK):
            for half in range(2):
                nc.scalar.activation(
                    pairs[half][:, t // 2, :, t % 2], ub[t][:, half * HALF : (half + 1) * HALF], ACT.Copy, scale=gain[:, t : t + 1]
                )
        z, z_codes, z_scales = [], [], []
        for half in range(2):
            z.append(held.tile([P, HALF, 2], F32, name=f"z{half}", tag=f"z{half}", align_bytes=64))
            words = pairs[half][:].rearrange("p u j e -> p (u j e)").bitcast(F32).rearrange("p (u j) -> p j u", u=2)
            nc.vector.tensor_copy(z[half][:], words)
        for half in range(2):
            z_codes.append(held.tile([P, HALF], U32, name=f"z_codes{half}", tag=f"z_codes{half}", align_bytes=64))
            z_scales.append(held.tile([P, HALF], U8, name=f"z_scales{half}", tag=f"z_scales{half}", align_bytes=64))
            nc.vector.quantize_mx(
                out=z_codes[half][:].bitcast(FP8X4),
                scales=z_scales[half][:],
                in_=z[half][:].rearrange("p j u -> p (j u)").bitcast(BF16),
            )
        cand_codes.append(held.tile([P, HALF], U32, name="cand_codes1", tag="z0", align_bytes=64))
        gather(cand_codes[1][:], x_table, entries(l_cand, HALF, HALF))

        scores, sent = [], []
        for c in range(BLOCKS):
            s = held.tile([P, S], F32, name=f"s{c}")
            for half in range(2):
                bank = psum.tile([P, HALF], F32, name=f"s_bank{c}_{half}", tag=f"product_bank{(2 * c + half) % BLOCKS}")
                nc.tensor.matmul_mx(
                    out=bank[:],
                    lhsT=cand_codes[c // 2][:, (c % 2) * P : (c % 2 + 1) * P].bitcast(FP8X4),
                    lhsT_scale=cand_scales[:, c * P : (c + 1) * P],
                    rhs=z_codes[half][:].bitcast(FP8X4),
                    rhs_scale=z_scales[half][:],
                    start=True,
                    stop=True,
                )
                nc.scalar.activation(s[:, half * HALF : (half + 1) * HALF], bank[:], ACT.Copy, scale=SIXTEENTH)
            ds = held.tile([P, DS_COLUMNS], F32, name=f"ds{c}")
            width = HALF if c == 0 else S
            for first in range(0, S, width):
                nc.vector.tensor_copy(ds[:].indirect(entries(l_n5, first, width)), s[:, first : first + width])
            scores.append(s)
            sent.append(ds)

        page_tags = ("z_codes1", "z_scales1", "z0", "last_page")
        for c in range(BLOCKS):
            s, ds = scores[c], sent[c]
            minus_s = held.tile([P, S], F32, name=f"minus_s{c}")
            nc.scalar.activation(minus_s[:], s[:], ACT.Copy, scale=-1.0)
            page = held.tile([P, U], F32, name=f"page{c}", tag=page_tags[c], align_bytes=64)
            difference = psum.tile([P, S], F32, name=f"difference{c}", tag=f"turn_bank{2 * (c % 2)}")
            for b in range(BLOCKS):
                cols = slice(b * P, (b + 1) * P)
                nc.tensor.matmul(difference[:, cols], minus_s[:, cols], identity[:], start=True, stop=False, is_transpose=True)
                nc.tensor.matmul(difference[:, cols], ds[:, cols], identity[:], start=False, stop=True, is_transpose=True)
            excess_turned = held.tile([P, S], F32, name=f"excess_turned{c}")
            nc.scalar.activation(excess_turned[:], difference[:], ACT.Relu)
            back = psum.tile([P, S], F32, name=f"back{c}", tag=f"turn_bank{2 * (c % 2) + 1}")
            for b in range(BLOCKS):
                cols = slice(b * P, (b + 1) * P)
                nc.tensor.transpose(back[:, cols], excess_turned[:, cols], identity[:])
            excess = held.tile([P, S], F32, name=f"excess{c}")
            nc.scalar.copy(excess[:], back[:])
            nc.vector.tensor_copy(page[:].indirect(l_n3[:]), ds[:, 0:S])
            nc.vector.tensor_tensor(page[:].indirect(l_n4[:]), s[:], excess[:], ALU.add)
            nc.sync.dma_start(out[c * P : (c + 1) * P, :], page[:])
